import numpy as np
import ml_dtypes


def mxq(x, axis, fmt="e4m3"):
    dtype, down = {"e4m3": (ml_dtypes.float8_e4m3fn, 7), "e5m2": (ml_dtypes.float8_e5m2, 14)}[fmt]
    v = np.moveaxis(np.asarray(x, np.float32).astype(ml_dtypes.bfloat16).astype(np.float64), axis, -1)
    blocks = v.reshape(v.shape[:-1] + (-1, 32))
    amax = np.abs(blocks).max(-1, keepdims=True)
    byte = np.maximum(np.where(amax > 0, np.frexp(amax)[1] - 1 + 127, 0) - down, 1)
    scale = np.exp2(byte - 127.0)
    codes = (blocks / scale).astype(np.float32).astype(dtype).astype(np.float64)
    return np.moveaxis((codes * scale).reshape(v.shape), -1, axis)


WIDE = False


def mx_kscale(k):
    if not WIDE:
        return np.ones(k)
    levels = np.array([10, -10, 5, -5, 0])
    if k % 512:
        return np.exp2(np.random.permutation(np.resize(levels, k // 32))).repeat(32)
    a = np.empty((k // 512, 16))
    for p in range(k // 512):
        a[p, :8] = np.random.permutation(np.resize(levels, 8))
        for g in range(8):
            far = levels[np.abs(levels - a[p, g]) >= 10]
            a[p, g + 8] = far[np.random.randint(len(far))]
    return np.exp2(a.ravel()).repeat(32)


BF16 = ml_dtypes.bfloat16


def bf(x):
    return np.asarray(x, np.float32).astype(BF16)


def f64(x):
    return np.asarray(x).astype(np.float64)


B, D, N, F, T, J, H = 4096, 512, 4, 512, 4, 8, 128
P = F // J
G = T * J * N


def softmax_last(z):
    e = np.exp(z - z.max(-1, keepdims=True))
    return e / e.sum(-1, keepdims=True)


def draw0():
    s, t = mx_kscale(D), mx_kscale(F)
    return {
        "x": bf(np.random.standard_normal((B, D)) * s),
        "we": bf(np.random.standard_normal((N, D, F)) * (1.4 / np.sqrt(D)) / s[:, None]),
        "be": bf(np.random.standard_normal((N, F)) * 0.3),
        "wg": bf(np.random.standard_normal((D, G)) * (1.5 / np.sqrt(D)) / s[:, None]),
        "a": bf(np.random.standard_normal((T, F)) * t),
        "wt": bf(np.random.standard_normal((T, F, H)) * (1.5 / np.sqrt(F)) / t[:, None]),
        "bt": bf(np.random.standard_normal((T, H)) * 0.3),
    }


def core(x, we, be, wg, a, wt, bt):
    h = np.maximum((mxq(f64(x), 1, "e4m3") @ mxq(f64(we), 1, "e4m3")) + f64(be)[:, None, :], 0.0)
    z = (f64(x) @ f64(wg)).reshape(B, T, J, N)
    gate = softmax_last(z)
    gate_t = gate.transpose(1, 0, 2, 3)
    h_blocks = h.reshape(N, B, J, P)
    m = gate_t[:, :, :, 0, None] * h_blocks[0][None]
    for n in range(1, N):
        m = m + gate_t[:, :, :, n, None] * h_blocks[n][None]
    m = m.reshape(T, B, F)
    u = f64(a)[:, None, :] * m
    return (mxq(u, 2, "e4m3") @ mxq(f64(wt), 1, "e4m3")) + f64(bt)[:, None, :]


def e4m3fn_bytes(y):
    return np.clip(np.asarray(y, np.float64), -448.0, 448.0).astype(np.float32).astype(ml_dtypes.float8_e4m3fn).view(np.uint8)


def e4m3fn_values(b):
    return np.asarray(b, np.uint8).view(ml_dtypes.float8_e4m3fn).astype(np.float64)


def setup_inputs():
    d = draw0()
    x0 = np.asarray(d['we']).astype(np.float64)
    s = (np.max(np.abs(x0), axis=(0, 2), keepdims=True) / 448.0).astype(np.float32)
    out = {}
    for k, v in d.items():
        if k == 'we':
            out['we_bytes'] = e4m3fn_bytes(x0 / s.astype(np.float64))
            out['we_scale'] = s
        else:
            out[k] = v
    return out


def reference(x, we_bytes, we_scale, be, wg, a, wt, bt):
    return core(x, e4m3fn_values(we_bytes) * we_scale.astype(np.float64), be, wg, a, wt, bt)

from contextlib import ExitStack

import concourse.mybir as mybir
from concourse.masks import make_identity

B, D, N, F, T, J, H = 4096, 512, 4, 512, 4, 8, 128
P = 128
Q = 4
C = 16
RT = B // P
BT = B // 512
FLOPS = 2 * B * D * N * F + 2 * B * D * T * J * N + 2 * T * B * F * H

F32 = mybir.dt.float32
BF16 = mybir.dt.bfloat16
U32 = mybir.dt.uint32
U8 = mybir.dt.uint8
FP8 = mybir.dt.float8_e4m3fn
FP8X4 = mybir.dt.float8_e4m3fn_x4
ADD = mybir.AluOpType.add
SUB = mybir.AluOpType.subtract
MULT = mybir.AluOpType.mult
MAX = mybir.AluOpType.max
AX = mybir.AxisListType.X
RELU = mybir.ActivationFunctionType.Relu
EXP = mybir.ActivationFunctionType.Exp
COPY = mybir.ActivationFunctionType.Copy

ORDER = (3, 0, 1, 2)
LEAD = 7
PLAN = {(n, t): ("M", "S", "GGGS"[t])[n] for n in range(3) for t in range(T)}


def tile_multigateexperttowers_t_kernel(tc, x, we_bytes, we_scale, be, wg, a, wt, bt, out):
    nc = tc.nc
    with ExitStack() as ctx:
        keep = ctx.enter_context(tc.tile_pool(name="keep", bufs=1))
        sb = ctx.enter_context(tc.tile_pool(name="sb", bufs=2))
        ps = ctx.enter_context(tc.psum_pool(name="ps", bufs=1))

        ident = keep.tile([P, P], F32, name="ident")
        make_identity(nc, ident[:])
        we_codes = keep.tile([P, N, F], U32, name="we_codes", align_bytes=64)
        we_sc = keep.tile([P, N, F], U8, name="we_sc", align_bytes=64)
        wt_codes = keep.tile([P, T, H], U32, name="wt_codes", align_bytes=64)
        wt_sc = keep.tile([P, T, H], U8, name="wt_sc", align_bytes=64)
        kscale = keep.tile([P, 4], F32, name="kscale")
        wg_sb = keep.tile([P, 4, T * J * N], BF16, name="wg_sb")
        be_bf = keep.tile([P, N, Q], BF16, name="be_bf")
        be_f = keep.tile([P, N, Q], F32, name="be_f")
        a_bf = keep.tile([P, T, Q], BF16, name="a_bf")
        a_f = keep.tile([P, T, Q], F32, name="a_f")
        bt_bf = keep.tile([P, T * H], BF16, name="bt_bf")
        bt_f = keep.tile([P, T * H], F32, name="bt_f")
        wt_raw = keep.tile([P, T, Q, H], BF16, name="wt_raw")

        we_view = we_bytes.rearrange("n (p t) f -> n p t f", t=4)
        we_raw = {}
        x_sb = {}

        def load_we(n):
            w = keep.tile([P, 4, F], U8, name="we_raw%d" % n)
            nc.sync.dma_start(out=w[:], in_=we_view[n])
            we_raw[n] = w

        def load_x(b):
            xs = sb.tile([P, 4, D], BF16, name="xs", tag="xs", bufs=3)
            nc.sync.dma_start(out=xs[:], in_=x[b * 512 : (b + 1) * 512, :].rearrange("(r p) k -> p r k", p=P))
            x_sb[b] = xs

        with tc.manual_schedule():
            xt_bf, xc, xs8, z_bank, zs, ex, sums, rec, gate = {}, {}, {}, {}, {}, {}, {}, {}, {}
            hid, h3t, d2t, bank, prod, u_bf, uc, us = {}, {}, {}, {}, {}, {}, {}, {}
            acc_t = {}

            nc.scalar.dma_start(out=kscale[:], in_=we_scale.rearrange("o (p t) z -> p (o t z)", t=4))
            load_we(3)
            load_x(0)
            load_we(0)
            nc.scalar.dma_start(out=be_bf[:], in_=be.rearrange("n (p q) -> p n q", q=Q))
            nc.scalar.dma_start(out=wg_sb[:], in_=wg.rearrange("(p t) c -> p t c", t=4))
            load_we(1)
            load_we(2)
            nc.scalar.dma_start(out=a_bf[:], in_=a.rearrange("t (p q) -> p t q", q=Q))
            load_x(1)
            nc.sync.dma_start(out=wt_raw[:], in_=wt.rearrange("t (p q) h -> p t q h", q=Q))
            nc.scalar.dma_start(out=bt_bf[:], in_=bt.rearrange("t h -> (t h)").partition_broadcast(P))

            def widen(n, on_vector):
                w = sb.tile([P, 4, F], BF16, name="we_wide", tag="we_wide", bufs=2)
                for t in range(4):
                    src = we_raw[n][:, t, :].bitcast(FP8)
                    if t in on_vector:
                        nc.vector.tensor_scalar(out=w[:, t, :], in0=src, scalar1=kscale[:, t : t + 1], scalar2=None, op0=MULT)
                    else:
                        nc.scalar.activation(out=w[:, t, :], in_=src, func=COPY, scale=kscale[:, t : t + 1])
                return w

            def quant_we(n, w):
                g = sb.tile([P, F, 4], BF16, name="we_grp", tag="we_grp", bufs=2, align_bytes=64)
                nc.vector.tensor_copy(out=g[:].rearrange("p (q m) t -> p q m t", q=Q), in_=w[:].rearrange("p t (m q) -> p q m t", q=Q))
                nc.vector.quantize_mx(out=we_codes[:, n, :].bitcast(FP8X4), scales=we_sc[:, n, :], in_=g[:].rearrange("p f t -> p (f t)"))

            def quant_wt(t):
                g = sb.tile([P, H, Q], BF16, name="wt_grp", tag="wt_grp", bufs=2, align_bytes=64)
                nc.vector.tensor_copy(out=g[:], in_=wt_raw[:, t, :, :].rearrange("p q h -> p h q"))
                nc.vector.quantize_mx(out=wt_codes[:, t, :].bitcast(FP8X4), scales=wt_sc[:, t, :], in_=g[:].rearrange("p h q -> p (h q)"))

            def turn_x(b, half):
                if half == 0:
                    xt_bf[b] = sb.tile([P, 512, 4], BF16, name="xt_bf", tag="xt_bf", bufs=2, align_bytes=64)
                pt = ps.tile([P, 2, 2, P], F32, name="misc", tag="misc", bufs=1)
                for r in range(2):
                    words = x_sb[b][:, half * 2 + r, :].bitcast(F32)
                    for u in range(2):
                        nc.tensor.transpose(pt[:, r, u, :], words[:, u::2], ident[:])
                dst = xt_bf[b][:, half * 256 : (half + 1) * 256, :].rearrange("p b t -> p (b t)").bitcast(F32)
                nc.scalar.copy(out=dst.rearrange("p (r b u) -> p r b u", r=2, u=2), in_=pt[:].rearrange("p r u b -> p r b u"))

            def quant_x(b):
                xc[b] = sb.tile([P, 512], U32, name="xc", tag="xc", bufs=2, align_bytes=64)
                xs8[b] = sb.tile([P, 512], U8, name="xs8", tag="xs8", bufs=2, align_bytes=64)
                nc.vector.quantize_mx(out=xc[b][:].bitcast(FP8X4), scales=xs8[b][:], in_=xt_bf[b][:].rearrange("p b t -> p (b t)"))

            def gate_logits(b):
                zb = ps.tile([P, 4, T * J * N], F32, name="misc", tag="misc", bufs=1)
                for r in range(4):
                    for t in range(4):
                        nc.tensor.matmul(zb[:, r, :], lhsT=xt_bf[b][:, r * P : (r + 1) * P, t], rhs=wg_sb[:, t, :], start=(t == 0), stop=(t == 3))
                groups = zb[:].rearrange("p r (g n) -> p (r g) n", n=N)
                mx = sb.tile([P, 128], F32, name="mx", tag="mx", bufs=2)
                nc.vector.tensor_reduce(out=mx[:], in_=groups, axis=AX, op=MAX)
                zs[b] = sb.tile([P, 128, N], F32, name="zs", tag="zs", bufs=2)
                nc.vector.tensor_tensor(out=zs[b][:], in0=groups, in1=mx[:].unsqueeze(2).to_broadcast([P, 128, N]), op=SUB)

            def gate_exp(b):
                ex[b] = sb.tile([P, 128, N], F32, name="ex", tag="ex", bufs=2)
                nc.scalar.activation(out=ex[b][:], in_=zs[b][:], func=EXP)

            def gate_sum(b):
                s2 = sb.tile([P, 128, 2], F32, name="s2", tag="s2", bufs=2)
                nc.gpsimd.tensor_tensor(out=s2[:], in0=ex[b][:, :, 0:2], in1=ex[b][:, :, 2:4], op=ADD)
                sums[b] = sb.tile([P, 128], F32, name="ssum", tag="ssum", bufs=2)
                nc.gpsimd.tensor_tensor(out=sums[b][:], in0=s2[:, :, 0], in1=s2[:, :, 1], op=ADD)

            def gate_rec(b):
                rec[b] = sb.tile([P, 128], F32, name="rec", tag="rec", bufs=2)
                nc.vector.reciprocal(out=rec[b][:], in_=sums[b][:])

            def gate_norm(b):
                gate[b] = sb.tile([P, 4, T, J, N], F32, name="gate", tag="gate", bufs=3)
                nc.gpsimd.tensor_tensor(out=gate[b][:].rearrange("p r t j n -> p (r t j) n"), in0=ex[b][:], in1=rec[b][:].unsqueeze(2).to_broadcast([P, 128, N]), op=MULT)

            def expert(c, qs):
                b, n = c // 4, ORDER[c % 4]
                if qs[0] == 0:
                    hid[(b, n)] = sb.tile([P, Q, 512], F32, name="hid%d" % n, tag="hid%d" % n, bufs=3 if n in (3, 0) else 2)
                for q in qs:
                    pm = ps.tile([P, 512], F32, name="mm", tag="mm", bufs=2)
                    cols = slice(q * P, (q + 1) * P)
                    nc.tensor.matmul_mx(out=pm[:], lhsT=we_codes[:, n, cols].bitcast(FP8X4), lhsT_scale=we_sc[:, n, cols],
                                        rhs=xc[b][:].bitcast(FP8X4), rhs_scale=xs8[b][:], start=True, stop=True)
                    if b == 0 and q % 2 == 1:
                        nc.vector.tensor_scalar(out=hid[(b, n)][:, q, :], in0=pm[:], scalar1=be_f[:, n, q : q + 1], scalar2=0.0, op0=ADD, op1=MAX)
                    else:
                        nc.scalar.activation(out=hid[(b, n)][:, q, :], in_=pm[:], func=RELU, bias=be_f[:, n, q : q + 1])

            def differ(k):
                b, n, q = k // 12, (k % 12) // 4, k % 4
                eng = nc.vector if b == 0 else nc.gpsimd
                eng.tensor_tensor(out=hid[(b, n)][:, q, :], in0=hid[(b, n)][:, q, :], in1=hid[(b, 3)][:, q, :], op=SUB)

            def turn_h(r, n):
                b, cols = r // 4, slice((r % 4) * P, (r % 4 + 1) * P)
                tag = {3: "ta", 2: "ta", 0: "tb", 1: "tc"}[n]
                pb = ps.tile([P, 512], F32, name=tag, tag=tag, bufs=1)
                for q in range(Q):
                    nc.tensor.transpose(pb[:, q * P : (q + 1) * P], hid[(b, n)][:, q, cols], ident[:])
                bank[(r, n)] = pb
                if n == 3:
                    h3t[r] = sb.tile([P, 512], F32, name="h3t", tag="h3t", bufs=2)
                    nc.scalar.copy(out=h3t[r][:], in_=pb[:])
                if n == 2:
                    d2t[r] = sb.tile([P, 512], F32, name="d2t", tag="d2t", bufs=2)
                    nc.scalar.copy(out=d2t[r][:], in_=pb[:])

            def product(r, n, t):
                if not (0 <= r < RT):
                    return
                plan = PLAN[(n, t)]
                g = gate[r // 4]
                src = d2t[r] if n == 2 else bank[(r, n)]
                pr = sb.tile([P, 512], F32, name="pr%d" % n, tag="pr%d" % n, bufs=6)
                prod[(r, n, t)] = pr
                if plan in ("V", "G"):
                    gb = g[:, r % 4, t, :, n].unsqueeze(1).unsqueeze(3).to_broadcast([P, Q, J, C])
                    eng = nc.vector if plan == "V" else nc.gpsimd
                    eng.tensor_tensor(out=pr[:].rearrange("p (q j c) -> p q j c", q=Q, j=J), in0=src[:].rearrange("p (q j c) -> p q j c", q=Q, j=J), in1=gb, op=MULT)
                    return
                sv = src[:].rearrange("p (q j c) -> p j q c", q=Q, j=J)
                dv = pr[:].rearrange("p (q j c) -> p j q c", q=Q, j=J)
                for j in range(J):
                    gcol = g[:, r % 4, t, j, n : n + 1]
                    if plan == "M":
                        hv = h3t[r][:].rearrange("p (q j c) -> p j q c", q=Q, j=J)
                        nc.vector.scalar_tensor_tensor(out=dv[:, j], in0=sv[:, j], scalar=gcol, in1=hv[:, j], op0=MULT, op1=ADD)
                    else:
                        nc.scalar.activation(out=dv[:, j], in_=sv[:, j], func=COPY, scale=gcol)

            def accumulate(r, t):
                ac = ps.tile([P, Q, P], F32, name="acc", tag="acc", bufs=2)
                parts = [prod[(r, 1, t)], prod[(r, 0, t)], prod[(r, 2, t)]]
                if PLAN[(0, t)] != "M":
                    parts.insert(0, h3t[r])
                for q in range(Q):
                    for k, pr in enumerate(parts):
                        nc.tensor.matmul(ac[:, q, :], lhsT=pr[:, q * P : (q + 1) * P], rhs=ident[:], start=(k == 0), stop=(k == len(parts) - 1), is_transpose=True)
                acc_t[(r, t)] = ac

            def drain(r, t):
                if t == 0:
                    u_bf[r] = sb.tile([P, T, P, Q], BF16, name="u_bf", tag="u_bf", bufs=2, align_bytes=64)
                nc.vector.tensor_tensor(out=u_bf[r][:, t, :, :], in0=acc_t[(r, t)][:].rearrange("p q b -> p b q"), in1=a_f[:, t, :].unsqueeze(1).to_broadcast([P, P, Q]), op=MULT)

            def quant_u(r):
                uc[r] = sb.tile([P, 512], U32, name="uc", tag="uc", bufs=2, align_bytes=64)
                us[r] = sb.tile([P, 512], U8, name="us", tag="us", bufs=2, align_bytes=64)
                nc.vector.quantize_mx(out=uc[r][:].bitcast(FP8X4), scales=us[r][:], in_=u_bf[r][:].rearrange("p t b q -> p (t b q)"))

            def tower(r):
                po = ps.tile([P, T * H], F32, name="misc", tag="misc", bufs=1)
                for t in range(T):
                    cols = slice(t * P, (t + 1) * P)
                    nc.tensor.matmul_mx(out=po[:, t * H : (t + 1) * H], lhsT=uc[r][:, cols].bitcast(FP8X4), lhsT_scale=us[r][:, cols],
                                        rhs=wt_codes[:, t, :].bitcast(FP8X4), rhs_scale=wt_sc[:, t, :], start=True, stop=True)
                ot = sb.tile([P, T, H], F32, name="ot", tag="ot", bufs=3)
                nc.vector.tensor_tensor(out=ot[:].rearrange("p t h -> p (t h)"), in0=po[:], in1=bt_f[:], op=ADD)
                nc.sync.dma_start(out=out[:, r * P : (r + 1) * P, :].rearrange("t b h -> b t h"), in_=ot[:])

            def step(i):
                c = i + LEAD
                live_c = 0 <= c < 4 * BT
                rn = i + 1
                live_n = 0 <= rn < RT
                live = 0 <= i < RT
                xb, xph = (i + 10) // 4, (i + 10) % 4
                live_x = 0 <= xb < BT
                if 1 <= i <= RT:
                    quant_u(i - 1)
                if live_x and xph == 2:
                    quant_x(xb)
                if live_x and xph == 3:
                    gate_exp(xb)
                    gate_sum(xb)
                if live_c:
                    expert(c, (0, 1))
                if live_n:
                    turn_h(rn, 3)
                for n in (1, 2, 0):
                    product(i, n, 3)
                if live:
                    accumulate(i, 0)
                    drain(i, 0)
                if live_x and xph == 3:
                    gate_rec(xb)
                    gate_norm(xb)
                if live_n:
                    turn_h(rn, 0)
                    turn_h(rn, 1)
                    product(rn, 1, 0)
                    product(rn, 0, 0)
                if live:
                    accumulate(i, 1)
                    drain(i, 1)
                if live_c:
                    expert(c, (2, 3))
                if 1 <= i <= RT:
                    tower(i - 1)
                if live_n:
                    turn_h(rn, 2)
                    product(rn, 2, 0)
                    product(rn, 1, 1)
                    product(rn, 0, 1)
                if live:
                    accumulate(i, 2)
                    drain(i, 2)
                if live_x and xph < 2:
                    turn_x(xb, xph)
                    if xph == 1 and xb + 2 < BT:
                        load_x(xb + 2)
                if live_x and xph == 2:
                    gate_logits(xb)
                if live_n:
                    product(rn, 2, 1)
                    product(rn, 1, 2)
                    product(rn, 0, 2)
                    product(rn, 2, 2)
                if live:
                    accumulate(i, 3)
                    drain(i, 3)
                ds = 3 * (i + 5)
                for k in range(ds, ds + 3):
                    if 12 <= k < 12 * BT:
                        differ(k)
                if live_c and c < 4 and c > 0:
                    for q in range(4):
                        differ((c - 1) * 4 + q)

            w3 = widen(3, (2, 3))
            w0 = widen(0, ())
            for i in range(-10, RT + 1):
                if i == -8:
                    nc.vector.tensor_copy(out=be_f[:], in_=be_bf[:])
                    quant_we(3, w3)
                step(i)
                if i == -8:
                    quant_we(0, w0)
                    w1 = widen(1, ())
                if i == -7:
                    quant_we(1, w1)
                    w2 = widen(2, ())
                if i == -6:
                    quant_we(2, w2)
                if i == -3:
                    nc.vector.tensor_copy(out=a_f[:], in_=a_bf[:])
                    nc.vector.tensor_copy(out=bt_f[:], in_=bt_bf[:])
                    for t in range(T):
                        quant_wt(t)
